import numpy as np
import ml_dtypes


def mxq(x, axis, fmt="e4m3"):
    dtype, down = {"e4m3": (ml_dtypes.float8_e4m3fn, 7), "e5m2": (ml_dtypes.float8_e5m2, 14)}[fmt]
    v = np.moveaxis(np.asarray(x, np.float32).astype(ml_dtypes.bfloat16).astype(np.float64), axis, -1)
    blocks = v.reshape(v.shape[:-1] + (-1, 32))
    amax = np.abs(blocks).max(-1, keepdims=True)
    byte = np.maximum(np.where(amax > 0, np.frexp(amax)[1] - 1 + 127, 0) - down, 1)
    scale = np.exp2(byte - 127.0)
    codes = (blocks / scale).astype(np.float32).astype(dtype).astype(np.float64)
    return np.moveaxis((codes * scale).reshape(v.shape), -1, axis)


WIDE = False


def mx_kscale(k):
    if not WIDE:
        return np.ones(k)
    levels = np.array([10, -10, 5, -5, 0])
    if k % 512:
        return np.exp2(np.random.permutation(np.resize(levels, k // 32))).repeat(32)
    a = np.empty((k // 512, 16))
    for p in range(k // 512):
        a[p, :8] = np.random.permutation(np.resize(levels, 8))
        for g in range(8):
            far = levels[np.abs(levels - a[p, g]) >= 10]
            a[p, g + 8] = far[np.random.randint(len(far))]
    return np.exp2(a.ravel()).repeat(32)


def f64(x):
    return np.asarray(x).astype(np.float64)


def striped(idx):
    return np.tile(idx.reshape(-1, 16).T, (8, 1)).astype(np.uint16)


def unstriped(offs):
    return offs[:16].T.reshape(-1).astype(np.int64)


def striped8(idx):
    return np.concatenate([x.reshape(-1, 16).T for x in idx]).astype(np.uint16)


def runs(offs, k):
    lists = np.stack([offs[16 * r : 16 * r + 16].T.reshape(-1) for r in range(8)]).astype(np.int64)
    return lists[np.arange(k) % 512 // 64]


def pack_weight(w):
    k, n = w.shape
    w = f64(np.asarray(w, np.float32).astype(ml_dtypes.bfloat16)).reshape(k // 32, 32, n)
    amax = np.abs(w).max(1)
    byte = np.clip(np.where(amax > 0, np.frexp(amax)[1] - 1 + 127 - 7, 1), 1, 254)
    scaled = (w * np.exp2(127.0 - byte)[:, None, :]).reshape(k, n).astype(np.float32)
    words = np.ascontiguousarray(scaled.reshape(k // 512, 128, 4, n).transpose(0, 1, 3, 2)).astype(ml_dtypes.float8_e4m3fn).view(np.uint8)
    return words, np.ascontiguousarray(byte.astype(np.uint8).reshape(k // 512, 16, n))


def unpack_weight(words, scales):
    g, p, n, _ = words.shape
    vals = np.ascontiguousarray(words).view(ml_dtypes.float8_e4m3fn).astype(np.float64) * np.repeat(np.exp2(scales.astype(np.float64) - 127.0), 8, axis=1)[..., None]
    return vals.transpose(0, 1, 3, 2).reshape(g * 512, n)


E2M1 = np.array([0.0, 0.5, 1.0, 1.5, 2.0, 3.0, 4.0, 6.0, -0.0, -0.5, -1.0, -1.5, -2.0, -3.0, -4.0, -6.0])


def pack_fp4(w):
    k, n = w.shape
    w = f64(np.asarray(w, np.float32).astype(ml_dtypes.bfloat16)).reshape(k // 32, 32, n)
    amax = np.abs(w).max(1)
    mant, ex = np.frexp(amax / 6.0)
    byte = np.clip(np.where(amax > 0, np.where(mant > 0.5, ex, ex - 1) + 127, 1), 1, 254)
    scaled = (w * np.exp2(127.0 - byte)[:, None, :]).reshape(k, n).astype(np.float32)
    c = np.ascontiguousarray(scaled.reshape(k // 512, 128, 4, n).transpose(0, 1, 3, 2)).astype(ml_dtypes.float4_e2m1fn).view(np.uint8) & 0xF
    words = (c[..., 0::2] | (c[..., 1::2] << 4)).reshape(k // 512, 128, 2 * n)
    return np.ascontiguousarray(words), np.ascontiguousarray(byte.astype(np.uint8).reshape(k // 512, 16, n))


def unpack_fp4(words, scales):
    g, _, n = scales.shape
    words = np.ascontiguousarray(words).reshape(g, 128, n, 2)
    nib = np.empty((g, 128, n, 4), np.uint8)
    nib[..., 0::2] = words & 0xF
    nib[..., 1::2] = words >> 4
    vals = E2M1[nib] * np.repeat(np.exp2(scales.astype(np.float64) - 127.0), 8, axis=1)[..., None]
    return vals.transpose(0, 1, 3, 2).reshape(g * 512, n)


def sigmoid(v):
    return 1.0 / (1.0 + np.exp(-np.maximum(v, -700.0)))

def planes(y):
    n, m = y.shape
    v = y.astype(np.float32).astype(ml_dtypes.bfloat16).astype(np.float64).reshape(n // 32, 32, m)
    top = np.abs(v).max(1)
    byte = np.clip(np.where(top > 0, np.frexp(top)[1] - 1 + 127 - 7, 1), 1, 254)
    codes = (v * np.exp2(127.0 - byte)[:, None, :]).reshape(n, m).astype(np.float32).astype(ml_dtypes.float8_e4m3fn).view(np.uint8)
    words = codes.reshape(n // 512, 128, 4, m).transpose(0, 1, 3, 2)
    return np.ascontiguousarray(words), np.ascontiguousarray(byte.astype(np.uint8).reshape(n // 512, 16, m))


K, T, S, N, H, W = 512, 2048, 512, 512, 512, 256


def setup_inputs():
    n = np.random.standard_normal
    s = mx_kscale(K)[:, None]
    u = mx_kscale(S)
    packed_xT = pack_weight(n((K, T)) * s)
    packed_w1 = pack_fp4(n((S, N)) / np.sqrt(S) / u[:, None])
    perm = np.stack([np.random.permutation(H) for _ in range(8)])
    perm2 = np.stack([np.random.permutation(H) for _ in range(8)])
    return {
        "x_words": packed_xT[0],
        "x_scales": packed_xT[1],
        "wa": (n((K, H)) / np.sqrt(K) / s).astype(np.float32),
        "gt": (np.random.uniform(0.5, 1.5, (S, 1)) * u[:, None]).astype(np.float32),
        "w1_words": packed_w1[0],
        "w1_scales": packed_w1[1],
        "offs": striped(np.random.permutation(T)[:S]),
        "n1": striped8(perm[:, :W]),
        "n2": striped8(perm[:, W:]),
        "n3": striped8(perm2[:, :W]),
        "n4": striped8(perm2[:, W:]),
    }


def reference(x_words, x_scales, wa, gt, w1_words, w1_scales, offs, n1, n2, n3, n4):
    xq = unpack_weight(x_words, x_scales)[:, unstriped(offs)]
    y = xq.T @ mxq(f64(wa), 0, "e4m3")
    pa = y[np.arange(S)[:, None], runs(n1, S)]
    pb = y[np.arange(S)[:, None], runs(n2, S)]
    ra = np.maximum(pa, pb)
    ds = y.copy()
    ds[np.arange(S)[:, None], runs(n1, S)] = ra
    z = f64(gt) * ds
    h = unpack_fp4(w1_words, w1_scales).T @ mxq(z, 0, "e4m3")
    pb2 = h[np.arange(N)[:, None], runs(n4, N)]
    pa2 = h[np.arange(N)[:, None], runs(n3, N)]
    rb = pb2 * sigmoid(pb2 - pa2)
    ra2 = pa2 * sigmoid(pa2 - pb2)
    ds2 = np.zeros((N, H))
    ds2[np.arange(N)[:, None], runs(n3, N)] = ra2
    out = ds2.copy()
    out[np.arange(N)[:, None], runs(n4, N)] = rb
    return (out,) + planes(out)

@@ -1,0 +1,230 @@
+from contextlib import ExitStack
+
+import concourse.mybir as mybir
+
+K, T, S, N, H, W = 512, 2048, 512, 512, 512, 256
+FLOPS = 2 * K * S * H + 2 * S * N * H
+
+F32 = mybir.dt.float32
+BF16 = mybir.dt.bfloat16
+I32 = mybir.dt.int32
+U32 = mybir.dt.uint32
+U16 = mybir.dt.uint16
+U8 = mybir.dt.uint8
+FP8X4 = mybir.dt.float8_e4m3fn_x4
+FP4X4 = mybir.dt.float4_e2m1fn_x4
+ALU = mybir.AluOpType
+ACT = mybir.ActivationFunctionType
+
+P = 128
+PACK = 4
+HALF = H // 2
+ORDER = (2, 0, 1, 3)
+WA_SPLIT = 160
+LAST_SPLIT = 320
+
+
+def tile_picked_tokfillduel_none_po_kernel(
+    tc, x_words, x_scales, wa, gt, w1_words, w1_scales, offs, n1, n2, n3, n4, out_0, out_1, out_2
+):
+    nc = tc.nc
+    with ExitStack() as ctx:
+        keep = ctx.enter_context(tc.tile_pool(name="keep", bufs=1))
+        psum = ctx.enter_context(tc.psum_pool(name="psum", bufs=1))
+
+        def sb(name, shape, dtype, tag=""):
+            return keep.tile(shape, dtype, name=name, tag=tag or name, align_bytes=64)
+
+        def load_scale_rows(queue, plane, rows):
+            for q in range(4):
+                queue.dma_start(out=plane[32 * q : 32 * q + 4, :].bitcast(I32), in_=rows[4 * q : 4 * q + 4, :].bitcast(I32))
+
+        def load_list(name, src):
+            lst = keep.tile([P, src.shape[1]], U16, name=name)
+            nc.sync.dma_start(lst[:], src)
+            return lst
+
+        warm = sb("warm", [P, 8], F32)
+        nc.gpsimd.memset(warm[:, 0:1], 0.0)
+        nc.scalar.activation(out=warm[:, 4:5], in_=warm[:, 0:1], func=ACT.Sigmoid)
+
+        xs_all = sb("xs_all", [P, T], U8)
+        nc.vector.memset(xs_all[:].bitcast(I32), 0)
+        w1s_raw = sb("w1s_raw", [P, N], U8)
+        nc.vector.memset(w1s_raw[:].bitcast(I32), 0)
+
+        offs_sb = load_list("offs_sb", offs)
+        xw_all = sb("xw_all", [P, T], U32)
+        nc.sync.dma_start(out=xw_all[:].bitcast(I32), in_=x_words[0].rearrange("p c r -> p (c r)").bitcast(I32))
+        load_scale_rows(nc.scalar, xs_all, x_scales[0])
+        wa_rows = wa.rearrange("(p j) c -> p j c", j=PACK)
+        wa_raw = []
+        for a in range(2):
+            raw = sb("wa_raw%d" % a, [P, PACK, HALF], F32)
+            nc.sync.dma_start(out=raw[:], in_=wa_rows[:, :, a * HALF : (a + 1) * HALF])
+            wa_raw.append(raw)
+        n1_sb = load_list("n1_sb", n1)
+        n2_sb = load_list("n2_sb", n2)
+        w1w_raw = sb("w1w_raw", [P, 2 * N], U8)
+        nc.sync.dma_start(out=w1w_raw[:].bitcast(I32), in_=w1_words[0].bitcast(I32))
+        load_scale_rows(nc.sync, w1s_raw, w1_scales[0])
+        gt_sb = sb("gt_sb", [P, PACK], F32)
+        nc.sync.dma_start(out=gt_sb[:], in_=gt.rearrange("(p t) o -> p (t o)", t=PACK))
+        n3_sb = load_list("n3_sb", n3)
+        n4_sb = load_list("n4_sb", n4)
+
+        xs_pick = sb("xs_pick", [P, S], U8)
+        nc.vector.tensor_copy(out=xs_pick[:], in_=xs_all[:].indirect(offs_sb[:]))
+        xs = sb("xs", [P, PACK, P], U8)
+        nc.vector.tensor_copy(out=xs[:], in_=xs_pick[:].rearrange("p (m t) -> p t m", t=PACK))
+        xw_pick = sb("xw_pick", [P, S], U32)
+        nc.vector.tensor_copy(out=xw_pick[:], in_=xw_all[:].indirect(offs_sb[:]))
+        xw = sb("xw", [P, PACK, P], U32)
+        nc.vector.tensor_copy(out=xw[:], in_=xw_pick[:].rearrange("p (m t) -> p t m", t=PACK))
+
+        wa_codes = sb("wa_codes", [P, H], U32)
+        wa_scales = sb("wa_scales", [P, H], U8)
+
+        def weave(copy, grouped, raw, c0, c1):
+            copy(
+                out=grouped[:, c0:c1, :].rearrange("p (c i) j -> p c j i", i=4),
+                in_=raw[:, :, c0:c1].rearrange("p j (c i) -> p c j i", i=4),
+            )
+
+        def quantize(codes, scales, grouped, a):
+            cols = slice(a * HALF, (a + 1) * HALF)
+            nc.vector.quantize_mx(
+                out=codes[:, cols].bitcast(FP8X4), scales=scales[:, cols], in_=grouped.rearrange("p c j -> p (c j)")
+            )
+
+        wa_bf = [sb("wa_bf%d" % a, [P, HALF, PACK], BF16) for a in range(2)]
+        weave(nc.scalar.copy, wa_bf[0], wa_raw[0], 0, HALF)
+        weave(nc.vector.tensor_copy, wa_bf[1], wa_raw[1], 0, WA_SPLIT)
+        weave(nc.scalar.copy, wa_bf[1], wa_raw[1], WA_SPLIT, HALF)
+        for a in range(2):
+            quantize(wa_codes, wa_scales, wa_bf[a][:], a)
+
+        def product(name, lhs, lhs_scale, codes, scales):
+            rows = {}
+            for i, t in enumerate(ORDER):
+                rows[t] = sb("%s%d" % (name, t), [P, H], F32)
+                pieces = [(0, HALF), (HALF, H)] if i == 0 else [(0, H)]
+                for a, (c0, c1) in enumerate(pieces):
+                    acc = psum.tile([P, c1 - c0], F32, name="%s_acc%d_%d" % (name, i, a), tag="bank%d_%d" % (i, a))
+                    nc.tensor.matmul_mx(
+                        out=acc[:], lhsT=lhs(t), lhsT_scale=lhs_scale[:, t, :],
+                        rhs=codes[:, c0:c1].bitcast(FP8X4), rhs_scale=scales[:, c0:c1], start=True, stop=True,
+                    )
+                    nc.scalar.copy(out=rows[t][:, c0:c1], in_=acc[:])
+            return rows
+
+        y = product("y", lambda t: xw[:, t, :].bitcast(FP8X4), xs, wa_codes, wa_scales)
+
+        w1w = sb("w1w", [P, PACK, 2 * P], U8)
+        for t in range(PACK):
+            nc.vector.tensor_copy(
+                out=w1w[:, t, :].rearrange("p (m e) -> p m e", e=2),
+                in_=w1w_raw[:].rearrange("p (m t e) -> p t m e", t=PACK, e=2)[:, t],
+            )
+        w1s = sb("w1s", [P, PACK, P], U8)
+        nc.vector.tensor_copy(out=w1s[:], in_=w1s_raw[:].rearrange("p (m t) -> p t m", t=PACK))
+
+        def gather(name, window, lst):
+            got = sb(name, [P, W], F32)
+            nc.vector.tensor_copy(out=got[:], in_=window[:].indirect(lst[:]))
+            return got
+
+        def round_plane(grouped, rows, t, last, scale):
+            c0 = LAST_SPLIT if last else 0
+            if last:
+                for a0, a1 in ((0, HALF), (HALF, LAST_SPLIT)):
+                    if scale is None:
+                        nc.vector.tensor_copy(out=grouped[:, a0:a1, t], in_=rows[:, a0:a1])
+                    else:
+                        nc.vector.tensor_scalar(
+                            out=grouped[:, a0:a1, t], in0=rows[:, a0:a1], scalar1=scale, scalar2=None, op0=ALU.mult
+                        )
+            if scale is None:
+                nc.scalar.copy(out=grouped[:, c0:H, t], in_=rows[:, c0:H])
+            else:
+                nc.scalar.activation(out=grouped[:, c0:H, t], in_=rows[:, c0:H], func=ACT.Copy, scale=scale)
+
+        z_bf = sb("z_bf", [P, H, PACK], BF16)
+        pa, pb, ra = {}, {}, {}
+
+        def fetch_a(t):
+            pa[t] = gather("pa%d" % t, y[t], n1_sb)
+
+        def fetch_b(t):
+            pb[t] = gather("pb%d" % t, y[t], n2_sb)
+
+        def larger(t):
+            ra[t] = sb("ra%d" % t, [P, W], F32, tag="y%d" % ORDER[0] if t == ORDER[-1] else "")
+            nc.vector.tensor_tensor(out=ra[t][:], in0=pa[t][:], in1=pb[t][:], op=ALU.max)
+
+        def put(t):
+            nc.vector.tensor_copy(out=y[t][:].indirect(n1_sb[:]), in_=ra[t][:])
+            round_plane(z_bf, y[t], t, t == ORDER[-1], gt_sb[:, t : t + 1])
+
+        t0, t1, t2, t3 = ORDER
+        for step, t in (
+            (fetch_a, t0), (fetch_b, t0), (fetch_a, t1), (larger, t0), (fetch_b, t1), (put, t0),
+            (fetch_a, t2), (larger, t1), (fetch_b, t2), (put, t1),
+            (fetch_a, t3), (fetch_b, t3), (larger, t2), (larger, t3), (put, t2), (put, t3),
+        ):
+            step(t)
+
+        z_codes = sb("z_codes", [P, H], U32)
+        z_scales = sb("z_scales", [P, H], U8)
+        for a in range(2):
+            quantize(z_codes, z_scales, z_bf[:, a * HALF : (a + 1) * HALF, :], a)
+
+        h = product("h", lambda t: w1w[:, t, :].bitcast(FP4X4), w1s, z_codes, z_scales)
+
+        o_bf = sb("o_bf", [P, H, PACK], BF16)
+        out_rows = out_0.rearrange("(p t) c -> p t c", t=PACK)
+        qa, qb, sa, sb2, res = {}, {}, {}, {}, {}
+
+        def fetch3(t):
+            qa[t] = gather("qa%d" % t, h[t], n3_sb)
+
+        def fetch4(t):
+            qb[t] = gather("qb%d" % t, h[t], n4_sb)
+
+        def gates(t):
+            d = sb("d%d" % t, [P, W], F32)
+            nc.vector.tensor_tensor(out=d[:], in0=qa[t][:], in1=qb[t][:], op=ALU.subtract)
+            sa[t] = sb("sa%d" % t, [P, W], F32)
+            nc.scalar.activation(out=sa[t][:], in_=d[:], func=ACT.Sigmoid)
+            sb2[t] = sb("sb%d" % t, [P, W], F32)
+            nc.scalar.activation(out=sb2[t][:], in_=d[:], func=ACT.Sigmoid, scale=-1.0)
+
+        def put3(t):
+            res[t] = sb("res%d" % t, [P, H], F32)
+            nc.vector.tensor_tensor(out=res[t][:].indirect(n3_sb[:]), in0=qa[t][:], in1=sa[t][:], op=ALU.mult)
+
+        def put4(t):
+            nc.vector.tensor_tensor(out=res[t][:].indirect(n4_sb[:]), in0=qb[t][:], in1=sb2[t][:], op=ALU.mult)
+            nc.sync.dma_start(out=out_rows[:, t, :], in_=res[t][:])
+            round_plane(o_bf, res[t], t, t == ORDER[-1], None)
+
+        for step, t in (
+            (fetch3, t0), (fetch4, t0), (fetch3, t1), (gates, t0), (fetch4, t1),
+            (put3, t0), (gates, t1), (put4, t0), (fetch3, t2), (fetch4, t2),
+            (put3, t1), (gates, t2), (put4, t1), (fetch3, t3), (fetch4, t3),
+            (put3, t2), (gates, t3), (put4, t2), (put3, t3), (put4, t3),
+        ):
+            step(t)
+
+        o_codes = sb("o_codes", [P, H], U32)
+        o_scales = sb("o_scales", [P, H], U8)
+        words_out = out_1[0].rearrange("p c r -> p (c r)").bitcast(I32)
+        for a in range(2):
+            cols = slice(a * HALF, (a + 1) * HALF)
+            quantize(o_codes, o_scales, o_bf[:, cols, :], a)
+            nc.sync.dma_start(out=words_out[:, cols], in_=o_codes[:, cols].bitcast(I32))
+        for q in range(4):
+            queue = nc.scalar if q % 2 == 0 else nc.sync
+            queue.dma_start(
+                out=out_2[0][4 * q : 4 * q + 4, :].bitcast(I32), in_=o_scales[32 * q : 32 * q + 4, :].bitcast(I32)
+            )

@@ -19,9 +19,10 @@ ACT = mybir.ActivationFunctionType
 P = 128
 PACK = 4
 HALF = H // 2
-ORDER = (2, 0, 1, 3)
-WA_SPLIT = 160
-LAST_SPLIT = 320
+ORDER = (0, 2, 3, 1)
+QUARTER = H // 4
+WA_PIECES = ((0, HALF), (HALF, HALF + QUARTER), (HALF + QUARTER, H))
+QUARTERS = tuple((c, c + QUARTER) for c in range(0, H, QUARTER))
 
 
 def tile_picked_tokfillduel_none_po_kernel(
@@ -44,25 +45,24 @@ def tile_picked_tokfillduel_none_po_kernel(
             nc.sync.dma_start(lst[:], src)
             return lst
 
-        warm = sb("warm", [P, 8], F32)
-        nc.gpsimd.memset(warm[:, 0:1], 0.0)
-        nc.scalar.activation(out=warm[:, 4:5], in_=warm[:, 0:1], func=ACT.Sigmoid)
-
         xs_all = sb("xs_all", [P, T], U8)
-        nc.vector.memset(xs_all[:].bitcast(I32), 0)
+        nc.vector.memset(xs_all[:, : T // 2].bitcast(I32), 0)
+        nc.gpsimd.memset(xs_all[:, T // 2 :].bitcast(I32), 0)
         w1s_raw = sb("w1s_raw", [P, N], U8)
         nc.vector.memset(w1s_raw[:].bitcast(I32), 0)
 
+        wa_rows = wa.rearrange("(p j) c -> p j c", j=PACK)
+
+        def load_wa(a):
+            raw = sb("wa_raw%d" % a, [P, PACK, HALF], F32)
+            nc.sync.dma_start(out=raw[:], in_=wa_rows[:, :, a * HALF : (a + 1) * HALF])
+            return raw
+
+        load_scale_rows(nc.scalar, xs_all, x_scales[0])
         offs_sb = load_list("offs_sb", offs)
         xw_all = sb("xw_all", [P, T], U32)
         nc.sync.dma_start(out=xw_all[:].bitcast(I32), in_=x_words[0].rearrange("p c r -> p (c r)").bitcast(I32))
-        load_scale_rows(nc.scalar, xs_all, x_scales[0])
-        wa_rows = wa.rearrange("(p j) c -> p j c", j=PACK)
-        wa_raw = []
-        for a in range(2):
-            raw = sb("wa_raw%d" % a, [P, PACK, HALF], F32)
-            nc.sync.dma_start(out=raw[:], in_=wa_rows[:, :, a * HALF : (a + 1) * HALF])
-            wa_raw.append(raw)
+        wa_raw = [load_wa(0), load_wa(1)]
         n1_sb = load_list("n1_sb", n1)
         n2_sb = load_list("n2_sb", n2)
         w1w_raw = sb("w1w_raw", [P, 2 * N], U8)
@@ -72,15 +72,10 @@ def tile_picked_tokfillduel_none_po_kernel(
         nc.sync.dma_start(out=gt_sb[:], in_=gt.rearrange("(p t) o -> p (t o)", t=PACK))
         n3_sb = load_list("n3_sb", n3)
         n4_sb = load_list("n4_sb", n4)
-
         xs_pick = sb("xs_pick", [P, S], U8)
         nc.vector.tensor_copy(out=xs_pick[:], in_=xs_all[:].indirect(offs_sb[:]))
         xs = sb("xs", [P, PACK, P], U8)
         nc.vector.tensor_copy(out=xs[:], in_=xs_pick[:].rearrange("p (m t) -> p t m", t=PACK))
-        xw_pick = sb("xw_pick", [P, S], U32)
-        nc.vector.tensor_copy(out=xw_pick[:], in_=xw_all[:].indirect(offs_sb[:]))
-        xw = sb("xw", [P, PACK, P], U32)
-        nc.vector.tensor_copy(out=xw[:], in_=xw_pick[:].rearrange("p (m t) -> p t m", t=PACK))
 
         wa_codes = sb("wa_codes", [P, H], U32)
         wa_scales = sb("wa_scales", [P, H], U8)
@@ -91,43 +86,41 @@ def tile_picked_tokfillduel_none_po_kernel(
                 in_=raw[:, :, c0:c1].rearrange("p j (c i) -> p c j i", i=4),
             )
 
-        def quantize(codes, scales, grouped, a):
-            cols = slice(a * HALF, (a + 1) * HALF)
+        def quantize(codes, scales, grouped, c0, c1):
             nc.vector.quantize_mx(
-                out=codes[:, cols].bitcast(FP8X4), scales=scales[:, cols], in_=grouped.rearrange("p c j -> p (c j)")
+                out=codes[:, c0:c1].bitcast(FP8X4),
+                scales=scales[:, c0:c1],
+                in_=grouped[:, c0:c1, :].rearrange("p c j -> p (c j)"),
             )
 
-        wa_bf = [sb("wa_bf%d" % a, [P, HALF, PACK], BF16) for a in range(2)]
-        weave(nc.scalar.copy, wa_bf[0], wa_raw[0], 0, HALF)
-        weave(nc.vector.tensor_copy, wa_bf[1], wa_raw[1], 0, WA_SPLIT)
-        weave(nc.scalar.copy, wa_bf[1], wa_raw[1], WA_SPLIT, HALF)
-        for a in range(2):
-            quantize(wa_codes, wa_scales, wa_bf[a][:], a)
+        xw_pick = sb("xw_pick", [P, S], U32, tag="xs_pick")
+        nc.vector.tensor_copy(out=xw_pick[:], in_=xw_all[:].indirect(offs_sb[:]))
+        xw = sb("xw", [P, PACK, P], U32)
+        nc.vector.tensor_copy(out=xw[:], in_=xw_pick[:].rearrange("p (m t) -> p t m", t=PACK))
+        wa_bf = sb("wa_bf", [P, H, PACK], BF16)
+        for a, (first, second) in enumerate(
+            ((nc.scalar.copy, nc.vector.tensor_copy), (nc.vector.tensor_copy, nc.scalar.copy))
+        ):
+            weave(first, wa_bf[:, a * HALF : (a + 1) * HALF, :], wa_raw[a], 0, QUARTER)
+            weave(second, wa_bf[:, a * HALF : (a + 1) * HALF, :], wa_raw[a], QUARTER, HALF)
+        for c0, c1 in WA_PIECES:
+            quantize(wa_codes, wa_scales, wa_bf, c0, c1)
 
-        def product(name, lhs, lhs_scale, codes, scales):
+        def product(name, lhs, lhs_scale, codes, scales, first_pieces):
             rows = {}
             for i, t in enumerate(ORDER):
                 rows[t] = sb("%s%d" % (name, t), [P, H], F32)
-                pieces = [(0, HALF), (HALF, H)] if i == 0 else [(0, H)]
+                pieces = first_pieces if i == 0 else [(0, H)]
                 for a, (c0, c1) in enumerate(pieces):
                     acc = psum.tile([P, c1 - c0], F32, name="%s_acc%d_%d" % (name, i, a), tag="bank%d_%d" % (i, a))
                     nc.tensor.matmul_mx(
-                        out=acc[:], lhsT=lhs(t), lhsT_scale=lhs_scale[:, t, :],
+                        out=acc[:], lhsT=lhs(t), lhsT_scale=lhs_scale(t),
                         rhs=codes[:, c0:c1].bitcast(FP8X4), rhs_scale=scales[:, c0:c1], start=True, stop=True,
                     )
                     nc.scalar.copy(out=rows[t][:, c0:c1], in_=acc[:])
             return rows
 
-        y = product("y", lambda t: xw[:, t, :].bitcast(FP8X4), xs, wa_codes, wa_scales)
-
-        w1w = sb("w1w", [P, PACK, 2 * P], U8)
-        for t in range(PACK):
-            nc.vector.tensor_copy(
-                out=w1w[:, t, :].rearrange("p (m e) -> p m e", e=2),
-                in_=w1w_raw[:].rearrange("p (m t e) -> p t m e", t=PACK, e=2)[:, t],
-            )
-        w1s = sb("w1s", [P, PACK, P], U8)
-        nc.vector.tensor_copy(out=w1s[:], in_=w1s_raw[:].rearrange("p (m t) -> p t m", t=PACK))
+        y = product("y", lambda t: xw[:, t, :].bitcast(FP8X4), lambda t: xs[:, t, :], wa_codes, wa_scales, WA_PIECES)
 
         def gather(name, window, lst):
             got = sb(name, [P, W], F32)
@@ -135,19 +128,16 @@ def tile_picked_tokfillduel_none_po_kernel(
             return got
 
         def round_plane(grouped, rows, t, last, scale):
-            c0 = LAST_SPLIT if last else 0
-            if last:
-                for a0, a1 in ((0, HALF), (HALF, LAST_SPLIT)):
-                    if scale is None:
-                        nc.vector.tensor_copy(out=grouped[:, a0:a1, t], in_=rows[:, a0:a1])
-                    else:
-                        nc.vector.tensor_scalar(
-                            out=grouped[:, a0:a1, t], in0=rows[:, a0:a1], scalar1=scale, scalar2=None, op0=ALU.mult
-                        )
-            if scale is None:
-                nc.scalar.copy(out=grouped[:, c0:H, t], in_=rows[:, c0:H])
-            else:
-                nc.scalar.activation(out=grouped[:, c0:H, t], in_=rows[:, c0:H], func=ACT.Copy, scale=scale)
+            for i, (c0, c1) in enumerate(QUARTERS if last else [(0, H)]):
+                dst, src = grouped[:, c0:c1, t], rows[:, c0:c1]
+                if last and i < 2 and scale is None:
+                    nc.vector.tensor_copy(out=dst, in_=src)
+                elif last and i < 2:
+                    nc.vector.tensor_scalar(out=dst, in0=src, scalar1=scale, scalar2=None, op0=ALU.mult)
+                elif scale is None:
+                    nc.scalar.copy(out=dst, in_=src)
+                else:
+                    nc.scalar.activation(out=dst, in_=src, func=ACT.Copy, scale=scale)
 
         z_bf = sb("z_bf", [P, H, PACK], BF16)
         pa, pb, ra = {}, {}, {}
@@ -174,12 +164,31 @@ def tile_picked_tokfillduel_none_po_kernel(
         ):
             step(t)
 
+        w1w = sb("w1w", [P, PACK, 2 * P], U8, tag="wa_bf")
+        nc.vector.tensor_copy(
+            out=w1w[:].rearrange("p t (m e) -> p t m e", e=2),
+            in_=w1w_raw[:].rearrange("p (m t e) -> p t m e", t=PACK, e=2),
+        )
+        w1s_view = w1s_raw[:].rearrange("p (m t) -> p t m", t=PACK)
+        w1s_first = sb("w1s_first", [P, P], U8, tag="pa%d" % t0)
+        nc.vector.tensor_copy(out=w1s_first[:], in_=w1s_view[:, t0])
+
         z_codes = sb("z_codes", [P, H], U32)
         z_scales = sb("z_scales", [P, H], U8)
-        for a in range(2):
-            quantize(z_codes, z_scales, z_bf[:, a * HALF : (a + 1) * HALF, :], a)
+        for c0, c1 in QUARTERS:
+            quantize(z_codes, z_scales, z_bf, c0, c1)
 
-        h = product("h", lambda t: w1w[:, t, :].bitcast(FP4X4), w1s, z_codes, z_scales)
+        w1s_rest = sb("w1s_rest", [P, PACK - 1, P], U8, tag="z_bf")
+        nc.vector.tensor_copy(out=w1s_rest[:], in_=w1s_view[:, 1:])
+
+        h = product(
+            "h",
+            lambda t: w1w[:, t, :].bitcast(FP4X4),
+            lambda t: w1s_first[:] if t == t0 else w1s_rest[:, t - 1, :],
+            z_codes,
+            z_scales,
+            QUARTERS,
+        )
 
         o_bf = sb("o_bf", [P, H, PACK], BF16)
         out_rows = out_0.rearrange("(p t) c -> p t c", t=PACK)
@@ -191,13 +200,21 @@ def tile_picked_tokfillduel_none_po_kernel(
         def fetch4(t):
             qb[t] = gather("qb%d" % t, h[t], n4_sb)
 
-        def gates(t):
-            d = sb("d%d" % t, [P, W], F32)
-            nc.vector.tensor_tensor(out=d[:], in0=qa[t][:], in1=qb[t][:], op=ALU.subtract)
+        diff = {}
+
+        def gate3(t):
+            diff[t] = sb("d%d" % t, [P, W], F32)
+            nc.vector.tensor_tensor(out=diff[t][:], in0=qa[t][:], in1=qb[t][:], op=ALU.subtract)
             sa[t] = sb("sa%d" % t, [P, W], F32)
-            nc.scalar.activation(out=sa[t][:], in_=d[:], func=ACT.Sigmoid)
-            sb2[t] = sb("sb%d" % t, [P, W], F32)
-            nc.scalar.activation(out=sb2[t][:], in_=d[:], func=ACT.Sigmoid, scale=-1.0)
+            nc.scalar.activation(out=sa[t][:], in_=diff[t][:], func=ACT.Sigmoid)
+
+        def gate4(t):
+            sb2[t] = sb("sb%d" % t, [P, W], F32, tag="sb%d" % t0 if t == t3 else "")
+            nc.scalar.activation(out=sb2[t][:], in_=diff[t][:], func=ACT.Sigmoid, scale=-1.0)
+
+        def gates(t):
+            gate3(t)
+            gate4(t)
 
         def put3(t):
             res[t] = sb("res%d" % t, [P, H], F32)
@@ -210,19 +227,19 @@ def tile_picked_tokfillduel_none_po_kernel(
 
         for step, t in (
             (fetch3, t0), (fetch4, t0), (fetch3, t1), (gates, t0), (fetch4, t1),
-            (put3, t0), (gates, t1), (put4, t0), (fetch3, t2), (fetch4, t2),
-            (put3, t1), (gates, t2), (put4, t1), (fetch3, t3), (fetch4, t3),
-            (put3, t2), (gates, t3), (put4, t2), (put3, t3), (put4, t3),
+            (fetch3, t2), (gates, t1), (fetch4, t2), (fetch3, t3), (gates, t2), (fetch4, t3),
+            (put3, t0), (gate3, t3), (put3, t1), (put4, t0), (gate4, t3), (put3, t2), (put4, t1),
+            (put3, t3), (put4, t2), (put4, t3),
         ):
             step(t)
 
         o_codes = sb("o_codes", [P, H], U32)
         o_scales = sb("o_scales", [P, H], U8)
         words_out = out_1[0].rearrange("p c r -> p (c r)").bitcast(I32)
-        for a in range(2):
-            cols = slice(a * HALF, (a + 1) * HALF)
-            quantize(o_codes, o_scales, o_bf[:, cols, :], a)
-            nc.sync.dma_start(out=words_out[:, cols], in_=o_codes[:, cols].bitcast(I32))
+        for c0, c1 in QUARTERS:
+            quantize(o_codes, o_scales, o_bf, c0, c1)
+            if c1 % HALF == 0:
+                nc.sync.dma_start(out=words_out[:, c1 - HALF : c1], in_=o_codes[:, c1 - HALF : c1].bitcast(I32))
         for q in range(4):
             queue = nc.scalar if q % 2 == 0 else nc.sync
             queue.dma_start(

@@ -46,8 +46,7 @@ def tile_picked_tokfillduel_none_po_kernel(
             return lst
 
         xs_all = sb("xs_all", [P, T], U8)
-        nc.vector.memset(xs_all[:, : T // 2].bitcast(I32), 0)
-        nc.gpsimd.memset(xs_all[:, T // 2 :].bitcast(I32), 0)
+        nc.vector.memset(xs_all[:].bitcast(I32), 0)
         w1s_raw = sb("w1s_raw", [P, N], U8)
         nc.vector.memset(w1s_raw[:].bitcast(I32), 0)
 
@@ -58,20 +57,22 @@ def tile_picked_tokfillduel_none_po_kernel(
             nc.sync.dma_start(out=raw[:], in_=wa_rows[:, :, a * HALF : (a + 1) * HALF])
             return raw
 
-        load_scale_rows(nc.scalar, xs_all, x_scales[0])
         offs_sb = load_list("offs_sb", offs)
+        wa_raw = [load_wa(0)]
+        load_scale_rows(nc.sync, xs_all, x_scales[0])
         xw_all = sb("xw_all", [P, T], U32)
         nc.sync.dma_start(out=xw_all[:].bitcast(I32), in_=x_words[0].rearrange("p c r -> p (c r)").bitcast(I32))
-        wa_raw = [load_wa(0), load_wa(1)]
+        wa_raw.append(load_wa(1))
         n1_sb = load_list("n1_sb", n1)
-        n2_sb = load_list("n2_sb", n2)
         w1w_raw = sb("w1w_raw", [P, 2 * N], U8)
         nc.sync.dma_start(out=w1w_raw[:].bitcast(I32), in_=w1_words[0].bitcast(I32))
+        n2_sb = load_list("n2_sb", n2)
         load_scale_rows(nc.sync, w1s_raw, w1_scales[0])
         gt_sb = sb("gt_sb", [P, PACK], F32)
         nc.sync.dma_start(out=gt_sb[:], in_=gt.rearrange("(p t) o -> p (t o)", t=PACK))
         n3_sb = load_list("n3_sb", n3)
         n4_sb = load_list("n4_sb", n4)
+
         xs_pick = sb("xs_pick", [P, S], U8)
         nc.vector.tensor_copy(out=xs_pick[:], in_=xs_all[:].indirect(offs_sb[:]))
         xs = sb("xs", [P, PACK, P], U8)
@@ -93,17 +94,16 @@ def tile_picked_tokfillduel_none_po_kernel(
                 in_=grouped[:, c0:c1, :].rearrange("p c j -> p (c j)"),
             )
 
-        xw_pick = sb("xw_pick", [P, S], U32, tag="xs_pick")
+        wa_bf = sb("wa_bf", [P, H, PACK], BF16)
+        weave(nc.scalar.copy, wa_bf[:, :HALF, :], wa_raw[0], 0, HALF)
+        quantize(wa_codes, wa_scales, wa_bf, *WA_PIECES[0])
+        xw_pick = sb("xw_pick", [P, S], U32)
         nc.vector.tensor_copy(out=xw_pick[:], in_=xw_all[:].indirect(offs_sb[:]))
+        weave(nc.vector.tensor_copy, wa_bf[:, HALF:, :], wa_raw[1], 0, QUARTER)
+        weave(nc.scalar.copy, wa_bf[:, HALF:, :], wa_raw[1], QUARTER, HALF)
         xw = sb("xw", [P, PACK, P], U32)
         nc.vector.tensor_copy(out=xw[:], in_=xw_pick[:].rearrange("p (m t) -> p t m", t=PACK))
-        wa_bf = sb("wa_bf", [P, H, PACK], BF16)
-        for a, (first, second) in enumerate(
-            ((nc.scalar.copy, nc.vector.tensor_copy), (nc.vector.tensor_copy, nc.scalar.copy))
-        ):
-            weave(first, wa_bf[:, a * HALF : (a + 1) * HALF, :], wa_raw[a], 0, QUARTER)
-            weave(second, wa_bf[:, a * HALF : (a + 1) * HALF, :], wa_raw[a], QUARTER, HALF)
-        for c0, c1 in WA_PIECES:
+        for c0, c1 in WA_PIECES[1:]:
             quantize(wa_codes, wa_scales, wa_bf, c0, c1)
 
         def product(name, lhs, lhs_scale, codes, scales, first_pieces):
@@ -204,7 +204,8 @@ def tile_picked_tokfillduel_none_po_kernel(
 
         def gate3(t):
             diff[t] = sb("d%d" % t, [P, W], F32)
-            nc.vector.tensor_tensor(out=diff[t][:], in0=qa[t][:], in1=qb[t][:], op=ALU.subtract)
+            engine = nc.vector if t == t3 else nc.gpsimd
+            engine.tensor_tensor(out=diff[t][:], in0=qa[t][:], in1=qb[t][:], op=ALU.subtract)
             sa[t] = sb("sa%d" % t, [P, W], F32)
             nc.scalar.activation(out=sa[t][:], in_=diff[t][:], func=ACT.Sigmoid)
 

from contextlib import ExitStack

import concourse.mybir as mybir

K, T, S, N, H, W = 512, 2048, 512, 512, 512, 256
FLOPS = 2 * K * S * H + 2 * S * N * H

F32 = mybir.dt.float32
BF16 = mybir.dt.bfloat16
I32 = mybir.dt.int32
U32 = mybir.dt.uint32
U16 = mybir.dt.uint16
U8 = mybir.dt.uint8
FP8X4 = mybir.dt.float8_e4m3fn_x4
FP4X4 = mybir.dt.float4_e2m1fn_x4
ALU = mybir.AluOpType
ACT = mybir.ActivationFunctionType

P = 128
PACK = 4
HALF = H // 2
ORDER = (0, 2, 3, 1)
QUARTER = H // 4
WA_PIECES = ((0, HALF), (HALF, HALF + QUARTER), (HALF + QUARTER, H))
QUARTERS = tuple((c, c + QUARTER) for c in range(0, H, QUARTER))


def tile_picked_tokfillduel_none_po_kernel(
    tc, x_words, x_scales, wa, gt, w1_words, w1_scales, offs, n1, n2, n3, n4, out_0, out_1, out_2
):
    nc = tc.nc
    with ExitStack() as ctx:
        keep = ctx.enter_context(tc.tile_pool(name="keep", bufs=1))
        psum = ctx.enter_context(tc.psum_pool(name="psum", bufs=1))

        def sb(name, shape, dtype, tag=""):
            return keep.tile(shape, dtype, name=name, tag=tag or name, align_bytes=64)

        def load_scale_rows(queue, plane, rows):
            for q in range(4):
                queue.dma_start(out=plane[32 * q : 32 * q + 4, :].bitcast(I32), in_=rows[4 * q : 4 * q + 4, :].bitcast(I32))

        def load_list(name, src):
            lst = keep.tile([P, src.shape[1]], U16, name=name)
            nc.sync.dma_start(lst[:], src)
            return lst

        xs_all = sb("xs_all", [P, T], U8)
        nc.vector.memset(xs_all[:].bitcast(I32), 0)
        w1s_raw = sb("w1s_raw", [P, N], U8)
        nc.vector.memset(w1s_raw[:].bitcast(I32), 0)

        wa_rows = wa.rearrange("(p j) c -> p j c", j=PACK)

        def load_wa(a):
            raw = sb("wa_raw%d" % a, [P, PACK, HALF], F32)
            nc.sync.dma_start(out=raw[:], in_=wa_rows[:, :, a * HALF : (a + 1) * HALF])
            return raw

        offs_sb = load_list("offs_sb", offs)
        wa_raw = [load_wa(0)]
        load_scale_rows(nc.sync, xs_all, x_scales[0])
        xw_all = sb("xw_all", [P, T], U32)
        nc.sync.dma_start(out=xw_all[:].bitcast(I32), in_=x_words[0].rearrange("p c r -> p (c r)").bitcast(I32))
        wa_raw.append(load_wa(1))
        n1_sb = load_list("n1_sb", n1)
        w1w_raw = sb("w1w_raw", [P, 2 * N], U8)
        nc.sync.dma_start(out=w1w_raw[:].bitcast(I32), in_=w1_words[0].bitcast(I32))
        n2_sb = load_list("n2_sb", n2)
        load_scale_rows(nc.sync, w1s_raw, w1_scales[0])
        gt_sb = sb("gt_sb", [P, PACK], F32)
        nc.sync.dma_start(out=gt_sb[:], in_=gt.rearrange("(p t) o -> p (t o)", t=PACK))
        n3_sb = load_list("n3_sb", n3)
        n4_sb = load_list("n4_sb", n4)

        xs_pick = sb("xs_pick", [P, S], U8)
        nc.vector.tensor_copy(out=xs_pick[:], in_=xs_all[:].indirect(offs_sb[:]))
        xs = sb("xs", [P, PACK, P], U8)
        nc.vector.tensor_copy(out=xs[:], in_=xs_pick[:].rearrange("p (m t) -> p t m", t=PACK))

        wa_codes = sb("wa_codes", [P, H], U32)
        wa_scales = sb("wa_scales", [P, H], U8)

        def weave(copy, grouped, raw, c0, c1):
            copy(
                out=grouped[:, c0:c1, :].rearrange("p (c i) j -> p c j i", i=4),
                in_=raw[:, :, c0:c1].rearrange("p j (c i) -> p c j i", i=4),
            )

        def quantize(codes, scales, grouped, c0, c1):
            nc.vector.quantize_mx(
                out=codes[:, c0:c1].bitcast(FP8X4),
                scales=scales[:, c0:c1],
                in_=grouped[:, c0:c1, :].rearrange("p c j -> p (c j)"),
            )

        wa_bf = sb("wa_bf", [P, H, PACK], BF16)
        weave(nc.scalar.copy, wa_bf[:, :HALF, :], wa_raw[0], 0, HALF)
        quantize(wa_codes, wa_scales, wa_bf, *WA_PIECES[0])
        xw_pick = sb("xw_pick", [P, S], U32)
        nc.vector.tensor_copy(out=xw_pick[:], in_=xw_all[:].indirect(offs_sb[:]))
        weave(nc.vector.tensor_copy, wa_bf[:, HALF:, :], wa_raw[1], 0, QUARTER)
        weave(nc.scalar.copy, wa_bf[:, HALF:, :], wa_raw[1], QUARTER, HALF)
        xw = sb("xw", [P, PACK, P], U32)
        nc.vector.tensor_copy(out=xw[:], in_=xw_pick[:].rearrange("p (m t) -> p t m", t=PACK))
        for c0, c1 in WA_PIECES[1:]:
            quantize(wa_codes, wa_scales, wa_bf, c0, c1)

        def product(name, lhs, lhs_scale, codes, scales, first_pieces):
            rows = {}
            for i, t in enumerate(ORDER):
                rows[t] = sb("%s%d" % (name, t), [P, H], F32)
                pieces = first_pieces if i == 0 else [(0, H)]
                for a, (c0, c1) in enumerate(pieces):
                    acc = psum.tile([P, c1 - c0], F32, name="%s_acc%d_%d" % (name, i, a), tag="bank%d_%d" % (i, a))
                    nc.tensor.matmul_mx(
                        out=acc[:], lhsT=lhs(t), lhsT_scale=lhs_scale(t),
                        rhs=codes[:, c0:c1].bitcast(FP8X4), rhs_scale=scales[:, c0:c1], start=True, stop=True,
                    )
                    nc.scalar.copy(out=rows[t][:, c0:c1], in_=acc[:])
            return rows

        y = product("y", lambda t: xw[:, t, :].bitcast(FP8X4), lambda t: xs[:, t, :], wa_codes, wa_scales, WA_PIECES)

        def gather(name, window, lst):
            got = sb(name, [P, W], F32)
            nc.vector.tensor_copy(out=got[:], in_=window[:].indirect(lst[:]))
            return got

        def round_plane(grouped, rows, t, last, scale):
            for i, (c0, c1) in enumerate(QUARTERS if last else [(0, H)]):
                dst, src = grouped[:, c0:c1, t], rows[:, c0:c1]
                if last and i < 2 and scale is None:
                    nc.vector.tensor_copy(out=dst, in_=src)
                elif last and i < 2:
                    nc.vector.tensor_scalar(out=dst, in0=src, scalar1=scale, scalar2=None, op0=ALU.mult)
                elif scale is None:
                    nc.scalar.copy(out=dst, in_=src)
                else:
                    nc.scalar.activation(out=dst, in_=src, func=ACT.Copy, scale=scale)

        z_bf = sb("z_bf", [P, H, PACK], BF16)
        pa, pb, ra = {}, {}, {}

        def fetch_a(t):
            pa[t] = gather("pa%d" % t, y[t], n1_sb)

        def fetch_b(t):
            pb[t] = gather("pb%d" % t, y[t], n2_sb)

        def larger(t):
            ra[t] = sb("ra%d" % t, [P, W], F32, tag="y%d" % ORDER[0] if t == ORDER[-1] else "")
            nc.vector.tensor_tensor(out=ra[t][:], in0=pa[t][:], in1=pb[t][:], op=ALU.max)

        def put(t):
            nc.vector.tensor_copy(out=y[t][:].indirect(n1_sb[:]), in_=ra[t][:])
            round_plane(z_bf, y[t], t, t == ORDER[-1], gt_sb[:, t : t + 1])

        t0, t1, t2, t3 = ORDER
        for step, t in (
            (fetch_a, t0), (fetch_b, t0), (fetch_a, t1), (larger, t0), (fetch_b, t1), (put, t0),
            (fetch_a, t2), (larger, t1), (fetch_b, t2), (put, t1),
            (fetch_a, t3), (fetch_b, t3), (larger, t2), (larger, t3), (put, t2), (put, t3),
        ):
            step(t)

        w1w = sb("w1w", [P, PACK, 2 * P], U8, tag="wa_bf")
        nc.vector.tensor_copy(
            out=w1w[:].rearrange("p t (m e) -> p t m e", e=2),
            in_=w1w_raw[:].rearrange("p (m t e) -> p t m e", t=PACK, e=2),
        )
        w1s_view = w1s_raw[:].rearrange("p (m t) -> p t m", t=PACK)
        w1s_first = sb("w1s_first", [P, P], U8, tag="pa%d" % t0)
        nc.vector.tensor_copy(out=w1s_first[:], in_=w1s_view[:, t0])

        z_codes = sb("z_codes", [P, H], U32)
        z_scales = sb("z_scales", [P, H], U8)
        for c0, c1 in QUARTERS:
            quantize(z_codes, z_scales, z_bf, c0, c1)

        w1s_rest = sb("w1s_rest", [P, PACK - 1, P], U8, tag="z_bf")
        nc.vector.tensor_copy(out=w1s_rest[:], in_=w1s_view[:, 1:])

        h = product(
            "h",
            lambda t: w1w[:, t, :].bitcast(FP4X4),
            lambda t: w1s_first[:] if t == t0 else w1s_rest[:, t - 1, :],
            z_codes,
            z_scales,
            QUARTERS,
        )

        o_bf = sb("o_bf", [P, H, PACK], BF16)
        out_rows = out_0.rearrange("(p t) c -> p t c", t=PACK)
        qa, qb, sa, sb2, res = {}, {}, {}, {}, {}

        def fetch3(t):
            qa[t] = gather("qa%d" % t, h[t], n3_sb)

        def fetch4(t):
            qb[t] = gather("qb%d" % t, h[t], n4_sb)

        diff = {}

        def gate3(t):
            diff[t] = sb("d%d" % t, [P, W], F32)
            engine = nc.vector if t == t3 else nc.gpsimd
            engine.tensor_tensor(out=diff[t][:], in0=qa[t][:], in1=qb[t][:], op=ALU.subtract)
            sa[t] = sb("sa%d" % t, [P, W], F32)
            nc.scalar.activation(out=sa[t][:], in_=diff[t][:], func=ACT.Sigmoid)

        def gate4(t):
            sb2[t] = sb("sb%d" % t, [P, W], F32, tag="sb%d" % t0 if t == t3 else "")
            nc.scalar.activation(out=sb2[t][:], in_=diff[t][:], func=ACT.Sigmoid, scale=-1.0)

        def gates(t):
            gate3(t)
            gate4(t)

        def put3(t):
            res[t] = sb("res%d" % t, [P, H], F32)
            nc.vector.tensor_tensor(out=res[t][:].indirect(n3_sb[:]), in0=qa[t][:], in1=sa[t][:], op=ALU.mult)

        def put4(t):
            nc.vector.tensor_tensor(out=res[t][:].indirect(n4_sb[:]), in0=qb[t][:], in1=sb2[t][:], op=ALU.mult)
            nc.sync.dma_start(out=out_rows[:, t, :], in_=res[t][:])
            round_plane(o_bf, res[t], t, t == ORDER[-1], None)

        for step, t in (
            (fetch3, t0), (fetch4, t0), (fetch3, t1), (gates, t0), (fetch4, t1),
            (fetch3, t2), (gates, t1), (fetch4, t2), (fetch3, t3), (gates, t2), (fetch4, t3),
            (put3, t0), (gate3, t3), (put3, t1), (put4, t0), (gate4, t3), (put3, t2), (put4, t1),
            (put3, t3), (put4, t2), (put4, t3),
        ):
            step(t)

        o_codes = sb("o_codes", [P, H], U32)
        o_scales = sb("o_scales", [P, H], U8)
        words_out = out_1[0].rearrange("p c r -> p (c r)").bitcast(I32)
        for c0, c1 in QUARTERS:
            quantize(o_codes, o_scales, o_bf, c0, c1)
            if c1 % HALF == 0:
                nc.sync.dma_start(out=words_out[:, c1 - HALF : c1], in_=o_codes[:, c1 - HALF : c1].bitcast(I32))
        for q in range(4):
            queue = nc.scalar if q % 2 == 0 else nc.sync
            queue.dma_start(
                out=out_2[0][4 * q : 4 * q + 4, :].bitcast(I32), in_=o_scales[32 * q : 32 * q + 4, :].bitcast(I32)
            )
